import numpy as np
import ml_dtypes


def mxq(x, axis, fmt="e4m3"):
    dtype, down = {"e4m3": (ml_dtypes.float8_e4m3fn, 7), "e5m2": (ml_dtypes.float8_e5m2, 14)}[fmt]
    v = np.moveaxis(np.asarray(x, np.float32).astype(ml_dtypes.bfloat16).astype(np.float64), axis, -1)
    blocks = v.reshape(v.shape[:-1] + (-1, 32))
    amax = np.abs(blocks).max(-1, keepdims=True)
    byte = np.maximum(np.where(amax > 0, np.frexp(amax)[1] - 1 + 127, 0) - down, 1)
    scale = np.exp2(byte - 127.0)
    codes = (blocks / scale).astype(np.float32).astype(dtype).astype(np.float64)
    return np.moveaxis((codes * scale).reshape(v.shape), -1, axis)


WIDE = False


def mx_kscale(k):
    if not WIDE:
        return np.ones(k)
    levels = np.array([10, -10, 5, -5, 0])
    if k % 512:
        return np.exp2(np.random.permutation(np.resize(levels, k // 32))).repeat(32)
    a = np.empty((k // 512, 16))
    for p in range(k // 512):
        a[p, :8] = np.random.permutation(np.resize(levels, 8))
        for g in range(8):
            far = levels[np.abs(levels - a[p, g]) >= 10]
            a[p, g + 8] = far[np.random.randint(len(far))]
    return np.exp2(a.ravel()).repeat(32)


def f64(x):
    return np.asarray(x).astype(np.float64)


def striped(idx):
    return np.tile(np.asarray(idx).reshape(-1, 16).T, (8, 1)).astype(np.uint16)


def unstriped(offs):
    return offs[:16].T.reshape(-1).astype(np.int64)


E2M1 = np.array([0.0, 0.5, 1.0, 1.5, 2.0, 3.0, 4.0, 6.0, -0.0, -0.5, -1.0, -1.5, -2.0, -3.0, -4.0, -6.0])


def pack_weight(w, fmt):
    k, n = w.shape
    w = f64(np.asarray(w, np.float32).astype(ml_dtypes.bfloat16)).reshape(k // 32, 32, n)
    amax = np.abs(w).max(1)
    if fmt == "e4m3":
        byte = np.frexp(amax)[1] - 1 + 127 - 7
    else:
        mant, ex = np.frexp(amax / 6.0)
        byte = np.where(mant > 0.5, ex, ex - 1) + 127
    byte = np.clip(np.where(amax > 0, byte, 1), 1, 254)
    scaled = (w * np.exp2(127.0 - byte)[:, None, :]).reshape(k, n).astype(np.float32)
    by_word = np.ascontiguousarray(scaled.reshape(k // 512, 128, 4, n).transpose(0, 1, 3, 2))
    if fmt == "e4m3":
        words = by_word.astype(ml_dtypes.float8_e4m3fn).view(np.uint8)
    else:
        c = by_word.astype(ml_dtypes.float4_e2m1fn).view(np.uint8) & 0xF
        words = (c[..., 0::2] | (c[..., 1::2] << 4)).reshape(k // 512, 128, 2 * n)
    return np.ascontiguousarray(words), np.ascontiguousarray(byte.astype(np.uint8).reshape(k // 512, 16, n))


def unpack_weight(words, scales, fmt):
    g, _, n = scales.shape
    words = np.ascontiguousarray(words).reshape(g, 128, n, -1)
    if fmt == "e4m3":
        vals = words.view(ml_dtypes.float8_e4m3fn).astype(np.float64)
    else:
        nib = np.empty((g, 128, n, 4), np.uint8)
        nib[..., 0::2] = words & 0xF
        nib[..., 1::2] = words >> 4
        vals = E2M1[nib]
    vals = vals * np.repeat(np.exp2(scales.astype(np.float64) - 127.0), 8, axis=1)[..., None]
    return vals.transpose(0, 1, 3, 2).reshape(g * 512, n)


B, N, T, D, NQ = 1, 1024, 4096, 1024, 128
SEG = 16


def setup_inputs():
    n = np.random.standard_normal
    pages = np.random.permutation(T // 16)[:B * N // 16]
    idx = (pages[:, None] * 16 + np.arange(16)[None, :]).reshape(-1)
    s = mx_kscale(D)[:, None]
    kp = pack_weight(n((D, T)) / s, "e2m1")
    return {
        "qT": (n((B, D, NQ)) * s * (1.00 / np.sqrt(D))).astype(np.float32),
        "k_words": np.ascontiguousarray(kp[0].reshape(1, 2, 128, T, 2).transpose(0, 2, 3, 1, 4)).reshape(1, 128, T, 4),
        "k_scales": kp[1],
        "iw": (np.random.uniform(0.2, 2.0, (B, NQ, 1))).astype(np.float32),
        "offs": striped(idx),
    }


def reference(qT, k_words, k_scales, iw, offs):
    idx = unstriped(offs)
    pick = lambda x, which: x[:, which].reshape(x.shape[0], B, -1).transpose(1, 0, 2)
    k = unpack_weight(k_words.reshape(1, 128, T, 2, 2).transpose(0, 3, 1, 2, 4).reshape(2, 128, 2 * T), k_scales, "e2m1")
    kg = pick(k, idx)
    qq = mxq(f64(qT), 1, "e4m3")
    a = qq.transpose(0, 2, 1) @ kg
    y = a.reshape(B, NQ, N // SEG, SEG).max(-1) * f64(iw)
    return y

@@ -1,0 +1,150 @@
+from contextlib import ExitStack
+
+import concourse.mybir as mybir
+
+F32 = mybir.dt.float32
+BF16 = mybir.dt.bfloat16
+I32 = mybir.dt.int32
+U32 = mybir.dt.uint32
+U16 = mybir.dt.uint16
+U8 = mybir.dt.uint8
+FP8X4 = mybir.dt.float8_e4m3fn_x4
+FP4X4 = mybir.dt.float4_e2m1fn_x4
+
+P = 128
+PACK = 4
+K_PASS = P * PACK
+PASSES = 2
+POOL = 4096
+SLOTS = 1024
+QUERIES = 128
+RUN = 16
+HALF = SLOTS // 2
+SCALE_ROWS = 16
+QUAD = 32
+
+FLOPS = 2 * PASSES * K_PASS * QUERIES * SLOTS
+
+PIECES = [(0, 512, 512), (512, 256, 128), (768, 256, 128)]
+
+
+def tile_attend_softmaxsim_kernel(tc, qT, k_words, k_scales, iw, offs, out):
+    nc = tc.nc
+    with ExitStack() as ctx:
+        sb = ctx.enter_context(tc.tile_pool(name="sb", bufs=1))
+        ps = ctx.enter_context(tc.psum_pool(name="ps", bufs=1))
+
+        offsets = sb.tile([P, SLOTS // 16], U16, name="offsets")
+        scale_pool = sb.tile([P, POOL], U8, name="scale_pool", align_bytes=64)
+        word_pool = sb.tile([P, POOL], I32, name="word_pool", align_bytes=64)
+        weight = sb.tile([P, 1], F32, name="weight")
+        q_raw = [sb.tile([P, PACK, QUERIES], F32, name="q_raw%d" % g, tag="shared%d" % g, align_bytes=64) for g in range(PASSES)]
+
+        nc.sync.dma_start(
+            out=scale_pool[0 : PASSES * SCALE_ROWS, :].bitcast(I32),
+            in_=k_scales.rearrange("o f t -> (o f) t").bitcast(I32),
+        )
+        nc.sync.dma_start(offsets[:], offs)
+        nc.sync.dma_start(out=word_pool[:], in_=k_words[0].rearrange("p t b -> p (t b)").bitcast(I32))
+        for g in range(PASSES):
+            nc.sync.dma_start(
+                out=q_raw[g][:],
+                in_=qT[0, g * K_PASS : (g + 1) * K_PASS, :].rearrange("(p j) w -> p j w", j=PACK),
+            )
+        nc.gpsimd.dma_start(out=weight[:], in_=iw[0])
+
+        nc.vector.memset(scale_pool[32:64, :].bitcast(I32), 0)
+        nc.vector.memset(scale_pool[64:128, :].bitcast(I32), 0)
+        k_plane = [sb.tile([P, SLOTS], U8, name="k_plane%d" % g, align_bytes=64) for g in range(PASSES)]
+        nc.vector.memset(k_plane[1][:].bitcast(I32), 0)
+
+        scale_listed = sb.tile([P, SLOTS], U8, name="scale_listed", align_bytes=64)
+        nc.vector.tensor_copy(out=scale_listed[:], in_=scale_pool[:].indirect(offsets[:]))
+        nc.vector.tensor_copy(out=k_plane[0][:].bitcast(I32), in_=scale_listed[:].bitcast(I32))
+        for g in range(PASSES):
+            for quad in range(1 - g, P // QUAD):
+                row = g * SCALE_ROWS + 4 * quad
+                nc.sync.dma_start(
+                    out=k_plane[g][QUAD * quad : QUAD * quad + 4, :].bitcast(I32),
+                    in_=scale_listed[row : row + 4, :].bitcast(I32),
+                )
+
+        q_grouped = [sb.tile([P, QUERIES, PACK], BF16, name="q_grouped%d" % g, align_bytes=64) for g in range(PASSES)]
+        q_codes = [sb.tile([P, QUERIES], U32, name="q_codes%d" % g, align_bytes=64) for g in range(PASSES)]
+        q_plane = [sb.tile([P, QUERIES], U8, name="q_plane%d" % g, align_bytes=64) for g in range(PASSES)]
+        for g in range(PASSES):
+            nc.scalar.copy(
+                out=q_grouped[g][:].rearrange("p (c i) t -> p c t i", i=4),
+                in_=q_raw[g][:].rearrange("p t (c i) -> p c t i", i=4),
+            )
+
+        def quantise(g):
+            nc.vector.quantize_mx(
+                out=q_codes[g][:].bitcast(FP8X4),
+                scales=q_plane[g][:],
+                in_=q_grouped[g][:].rearrange("p w j -> p (w j)"),
+            )
+
+        pairs = [
+            sb.tile([P, HALF], U32, name="pairs0", align_bytes=64),
+            sb.tile([P, HALF], U32, name="pairs1", tag="shared1", align_bytes=64),
+        ]
+
+        def gather(h):
+            nc.vector.tensor_copy(
+                out=pairs[h][:],
+                in_=word_pool[:].bitcast(U32).indirect(offsets[:, h * HALF // 16 : (h + 1) * HALF // 16]),
+            )
+
+        k_codes = [
+            sb.tile([P, PASSES, 2 * n], U8, name="k_codes%d" % s, tag="shared0" if s == 0 else "k_codes%d" % s, align_bytes=64)
+            for s, n, w in PIECES
+        ]
+        scores = [ps.tile([P, 512], F32, name="scores%d" % s) for s, n, w in PIECES]
+        best = sb.tile([P, SLOTS // RUN], F32, name="best")
+        result = sb.tile([P, SLOTS // RUN], F32, name="result")
+
+        def part(i):
+            first, n, width = PIECES[i]
+            h, at = divmod(first, HALF)
+            nc.vector.tensor_copy(
+                out=k_codes[i][:].bitcast(U16),
+                in_=pairs[h][:, at : at + n].bitcast(U16).rearrange("p (n g) -> p g n", g=PASSES),
+            )
+
+        def multiply(i):
+            first, n, width = PIECES[i]
+            for c in range(0, n, width):
+                for g in range(PASSES):
+                    nc.tensor.matmul_mx(
+                        out=scores[i][:, c : c + width],
+                        lhsT=q_codes[g][:].bitcast(FP8X4),
+                        lhsT_scale=q_plane[g][:],
+                        rhs=k_codes[i][:, g, 2 * c : 2 * (c + width)].bitcast(FP4X4),
+                        rhs_scale=k_plane[g][:, first + c : first + c + width],
+                        start=(g == 0),
+                        stop=(g == PASSES - 1),
+                    )
+
+        def largest(i):
+            first, n, width = PIECES[i]
+            nc.vector.tensor_reduce(
+                out=best[:, first // RUN : (first + n) // RUN],
+                in_=scores[i][:, 0:n].rearrange("p (j r) -> p j r", r=RUN),
+                axis=mybir.AxisListType.X,
+                op=mybir.AluOpType.max,
+            )
+
+        gather(0)
+        quantise(0)
+        part(0)
+        quantise(1)
+        multiply(0)
+        gather(1)
+        for i in (1, 2):
+            part(i)
+            multiply(i)
+        for i in range(len(PIECES)):
+            largest(i)
+        nc.vector.tensor_scalar_mul(result[:], best[:], weight[:, 0:1])
+        nc.sync.dma_start(out=out[0], in_=result[:])

@@ -25,8 +25,6 @@ QUAD = 32
 
 FLOPS = 2 * PASSES * K_PASS * QUERIES * SLOTS
 
-PIECES = [(0, 512, 512), (512, 256, 128), (768, 256, 128)]
-
 
 def tile_attend_softmaxsim_kernel(tc, qT, k_words, k_scales, iw, offs, out):
     nc = tc.nc
@@ -37,8 +35,7 @@ def tile_attend_softmaxsim_kernel(tc, qT, k_words, k_scales, iw, offs, out):
         offsets = sb.tile([P, SLOTS // 16], U16, name="offsets")
         scale_pool = sb.tile([P, POOL], U8, name="scale_pool", align_bytes=64)
         word_pool = sb.tile([P, POOL], I32, name="word_pool", align_bytes=64)
-        weight = sb.tile([P, 1], F32, name="weight")
-        q_raw = [sb.tile([P, PACK, QUERIES], F32, name="q_raw%d" % g, tag="shared%d" % g, align_bytes=64) for g in range(PASSES)]
+        q_raw = [sb.tile([P, PACK, QUERIES], F32, name="q_raw%d" % g, tag="raw%d" % g, align_bytes=64) for g in range(PASSES)]
 
         nc.sync.dma_start(
             out=scale_pool[0 : PASSES * SCALE_ROWS, :].bitcast(I32),
@@ -51,7 +48,6 @@ def tile_attend_softmaxsim_kernel(tc, qT, k_words, k_scales, iw, offs, out):
                 out=q_raw[g][:],
                 in_=qT[0, g * K_PASS : (g + 1) * K_PASS, :].rearrange("(p j) w -> p j w", j=PACK),
             )
-        nc.gpsimd.dma_start(out=weight[:], in_=iw[0])
 
         nc.vector.memset(scale_pool[32:64, :].bitcast(I32), 0)
         nc.vector.memset(scale_pool[64:128, :].bitcast(I32), 0)
@@ -69,7 +65,7 @@ def tile_attend_softmaxsim_kernel(tc, qT, k_words, k_scales, iw, offs, out):
                     in_=scale_listed[row : row + 4, :].bitcast(I32),
                 )
 
-        q_grouped = [sb.tile([P, QUERIES, PACK], BF16, name="q_grouped%d" % g, align_bytes=64) for g in range(PASSES)]
+        q_grouped = [sb.tile([P, QUERIES, PACK], BF16, name="q_grouped%d" % g, tag="grouped%d" % g, align_bytes=64) for g in range(PASSES)]
         q_codes = [sb.tile([P, QUERIES], U32, name="q_codes%d" % g, align_bytes=64) for g in range(PASSES)]
         q_plane = [sb.tile([P, QUERIES], U8, name="q_plane%d" % g, align_bytes=64) for g in range(PASSES)]
         for g in range(PASSES):
@@ -85,66 +81,64 @@ def tile_attend_softmaxsim_kernel(tc, qT, k_words, k_scales, iw, offs, out):
                 in_=q_grouped[g][:].rearrange("p w j -> p (w j)"),
             )
 
-        pairs = [
-            sb.tile([P, HALF], U32, name="pairs0", align_bytes=64),
-            sb.tile([P, HALF], U32, name="pairs1", tag="shared1", align_bytes=64),
-        ]
-
-        def gather(h):
+        def gather(h, tag):
+            listed = sb.tile([P, HALF], U32, name="pairs%d" % h, tag=tag, align_bytes=64)
             nc.vector.tensor_copy(
-                out=pairs[h][:],
+                out=listed[:],
                 in_=word_pool[:].bitcast(U32).indirect(offsets[:, h * HALF // 16 : (h + 1) * HALF // 16]),
             )
+            return listed
 
-        k_codes = [
-            sb.tile([P, PASSES, 2 * n], U8, name="k_codes%d" % s, tag="shared0" if s == 0 else "k_codes%d" % s, align_bytes=64)
-            for s, n, w in PIECES
-        ]
-        scores = [ps.tile([P, 512], F32, name="scores%d" % s) for s, n, w in PIECES]
         best = sb.tile([P, SLOTS // RUN], F32, name="best")
         result = sb.tile([P, SLOTS // RUN], F32, name="result")
 
-        def part(i):
-            first, n, width = PIECES[i]
-            h, at = divmod(first, HALF)
-            nc.vector.tensor_copy(
-                out=k_codes[i][:].bitcast(U16),
-                in_=pairs[h][:, at : at + n].bitcast(U16).rearrange("p (n g) -> p g n", g=PASSES),
+        def product(bank, g, codes, first, width, start):
+            nc.tensor.matmul_mx(
+                out=bank,
+                lhsT=q_codes[g][:].bitcast(FP8X4),
+                lhsT_scale=q_plane[g][:],
+                rhs=codes.bitcast(FP4X4),
+                rhs_scale=k_plane[g][:, first : first + width],
+                start=start,
+                stop=not start,
             )
 
-        def multiply(i):
-            first, n, width = PIECES[i]
-            for c in range(0, n, width):
-                for g in range(PASSES):
-                    nc.tensor.matmul_mx(
-                        out=scores[i][:, c : c + width],
-                        lhsT=q_codes[g][:].bitcast(FP8X4),
-                        lhsT_scale=q_plane[g][:],
-                        rhs=k_codes[i][:, g, 2 * c : 2 * (c + width)].bitcast(FP4X4),
-                        rhs_scale=k_plane[g][:, first + c : first + c + width],
-                        start=(g == 0),
-                        stop=(g == PASSES - 1),
-                    )
-
-        def largest(i):
-            first, n, width = PIECES[i]
+        def largest(bank, first, n):
             nc.vector.tensor_reduce(
                 out=best[:, first // RUN : (first + n) // RUN],
-                in_=scores[i][:, 0:n].rearrange("p (j r) -> p j r", r=RUN),
+                in_=bank[:, 0:n].rearrange("p (j r) -> p j r", r=RUN),
                 axis=mybir.AxisListType.X,
                 op=mybir.AluOpType.max,
             )
 
-        gather(0)
+        front_bank = ps.tile([P, 512], F32, name="front_bank")
+        pairs = gather(0, "pairs0")
         quantise(0)
-        part(0)
+        front = sb.tile([P, PASSES, 2 * HALF], U8, name="front", tag="raw0", align_bytes=64)
+        nc.vector.tensor_copy(out=front[:].bitcast(U16), in_=pairs[:].bitcast(U16).rearrange("p (n g) -> p g n", g=PASSES))
         quantise(1)
-        multiply(0)
-        gather(1)
-        for i in (1, 2):
-            part(i)
-            multiply(i)
-        for i in range(len(PIECES)):
-            largest(i)
+        weight = sb.tile([P, 1], F32, name="weight", tag="grouped0", align_bytes=64)
+        nc.sync.dma_start(out=weight[:], in_=iw[0])
+        for g in range(PASSES):
+            product(front_bank[:], g, front[:, g, :], 0, HALF, g == 0)
+
+        pairs = gather(1, "raw1")
+        banks = [ps.tile([P, 512], F32, name="back_bank%d" % i) for i in range(3)]
+        place = {0: (0, 0), 128: (0, 128), 256: (1, 0), 384: (2, 0)}
+        for first, n in ((0, 128), (128, 128), (256, 256)):
+            back = sb.tile([P, PASSES, 2 * n], U8, name="back%d" % first, align_bytes=64)
+            nc.vector.tensor_copy(
+                out=back[:].bitcast(U16),
+                in_=pairs[:, first : first + n].bitcast(U16).rearrange("p (n g) -> p g n", g=PASSES),
+            )
+            for c in range(0, n, 128):
+                bank, at = place[first + c]
+                for g in (1, 0):
+                    product(banks[bank][:, at : at + 128], g, back[:, g, 2 * c : 2 * c + 256], HALF + first + c, 128, g == 1)
+
+        largest(front_bank, 0, HALF)
+        largest(banks[0], HALF, 256)
+        largest(banks[1], HALF + 256, 128)
+        largest(banks[2], HALF + 384, 128)
         nc.vector.tensor_scalar_mul(result[:], best[:], weight[:, 0:1])
         nc.sync.dma_start(out=out[0], in_=result[:])

@@ -114,8 +114,20 @@ def tile_attend_softmaxsim_kernel(tc, qT, k_words, k_scales, iw, offs, out):
         front_bank = ps.tile([P, 512], F32, name="front_bank")
         pairs = gather(0, "pairs0")
         quantise(0)
+        warm_bank = ps.tile([P, 512], F32, name="warm_bank")
+        nc.tensor.matmul_mx(
+            out=warm_bank[:],
+            lhsT=q_codes[0][:].bitcast(FP8X4),
+            lhsT_scale=q_plane[0][:],
+            rhs=pairs[:, 0:256].bitcast(FP4X4),
+            rhs_scale=k_plane[0][:, 0:512],
+            start=True,
+            stop=True,
+        )
         front = sb.tile([P, PASSES, 2 * HALF], U8, name="front", tag="raw0", align_bytes=64)
-        nc.vector.tensor_copy(out=front[:].bitcast(U16), in_=pairs[:].bitcast(U16).rearrange("p (n g) -> p g n", g=PASSES))
+        halves = pairs[:].bitcast(U16).rearrange("p (n g) -> p g n", g=PASSES)
+        for g in range(PASSES):
+            nc.vector.tensor_copy(out=front[:, g, :].bitcast(U16), in_=halves[:, g, :])
         quantise(1)
         weight = sb.tile([P, 1], F32, name="weight", tag="grouped0", align_bytes=64)
         nc.sync.dma_start(out=weight[:], in_=iw[0])

@@ -22,6 +22,7 @@ RUN = 16
 HALF = SLOTS // 2
 SCALE_ROWS = 16
 QUAD = 32
+LEAD = 1280
 
 FLOPS = 2 * PASSES * K_PASS * QUERIES * SLOTS
 
@@ -37,32 +38,36 @@ def tile_attend_softmaxsim_kernel(tc, qT, k_words, k_scales, iw, offs, out):
         word_pool = sb.tile([P, POOL], I32, name="word_pool", align_bytes=64)
         q_raw = [sb.tile([P, PACK, QUERIES], F32, name="q_raw%d" % g, tag="raw%d" % g, align_bytes=64) for g in range(PASSES)]
 
-        nc.sync.dma_start(
-            out=scale_pool[0 : PASSES * SCALE_ROWS, :].bitcast(I32),
-            in_=k_scales.rearrange("o f t -> (o f) t").bitcast(I32),
-        )
+        nc.vector.memset(scale_pool[:].bitcast(I32), 0)
+        words = k_words[0].rearrange("p t b -> p (t b)").bitcast(I32)
         nc.sync.dma_start(offsets[:], offs)
-        nc.sync.dma_start(out=word_pool[:], in_=k_words[0].rearrange("p t b -> p (t b)").bitcast(I32))
+        nc.sync.dma_start(out=word_pool[:, 0:LEAD], in_=words[:, 0:LEAD])
+        nc.sync.dma_start(
+            out=scale_pool[QUAD : 3 * QUAD : 2, :].bitcast(I32),
+            in_=k_scales.rearrange("o f t -> f o t").bitcast(I32),
+        )
+        nc.sync.dma_start(out=word_pool[:, LEAD:POOL], in_=words[:, LEAD:POOL])
         for g in range(PASSES):
             nc.sync.dma_start(
                 out=q_raw[g][:],
                 in_=qT[0, g * K_PASS : (g + 1) * K_PASS, :].rearrange("(p j) w -> p j w", j=PACK),
             )
 
-        nc.vector.memset(scale_pool[32:64, :].bitcast(I32), 0)
-        nc.vector.memset(scale_pool[64:128, :].bitcast(I32), 0)
-        k_plane = [sb.tile([P, SLOTS], U8, name="k_plane%d" % g, align_bytes=64) for g in range(PASSES)]
-        nc.vector.memset(k_plane[1][:].bitcast(I32), 0)
+        k_plane = [sb.tile([P, PASSES * HALF], U8, name="k_plane%d" % h, align_bytes=64) for h in range(2)]
+        for h in range(2):
+            nc.vector.memset(k_plane[h][:].bitcast(I32), 0)
 
-        scale_listed = sb.tile([P, SLOTS], U8, name="scale_listed", align_bytes=64)
-        nc.vector.tensor_copy(out=scale_listed[:], in_=scale_pool[:].indirect(offsets[:]))
-        nc.vector.tensor_copy(out=k_plane[0][:].bitcast(I32), in_=scale_listed[:].bitcast(I32))
-        for g in range(PASSES):
-            for quad in range(1 - g, P // QUAD):
-                row = g * SCALE_ROWS + 4 * quad
+        for h in range(2):
+            scale_listed = sb.tile([P, HALF], U8, name="scale_listed%d" % h, align_bytes=64)
+            nc.vector.tensor_copy(
+                out=scale_listed[:],
+                in_=scale_pool[:].indirect(offsets[:, h * HALF // 16 : (h + 1) * HALF // 16]),
+            )
+            for quad in (0, 2, 1, 3):
+                row = QUAD + 16 * quad
                 nc.sync.dma_start(
-                    out=k_plane[g][QUAD * quad : QUAD * quad + 4, :].bitcast(I32),
-                    in_=scale_listed[row : row + 4, :].bitcast(I32),
+                    out=k_plane[h][QUAD * quad : QUAD * quad + 4, :].bitcast(I32),
+                    in_=scale_listed[row : row + 16 : 2, :].bitcast(I32),
                 )
 
         q_grouped = [sb.tile([P, QUERIES, PACK], BF16, name="q_grouped%d" % g, tag="grouped%d" % g, align_bytes=64) for g in range(PASSES)]
@@ -98,7 +103,7 @@ def tile_attend_softmaxsim_kernel(tc, qT, k_words, k_scales, iw, offs, out):
                 lhsT=q_codes[g][:].bitcast(FP8X4),
                 lhsT_scale=q_plane[g][:],
                 rhs=codes.bitcast(FP4X4),
-                rhs_scale=k_plane[g][:, first : first + width],
+                rhs_scale=k_plane[first // HALF][:, g * HALF + first % HALF : g * HALF + first % HALF + width],
                 start=start,
                 stop=not start,
             )

@@ -31,17 +31,18 @@ def tile_attend_softmaxsim_kernel(tc, qT, k_words, k_scales, iw, offs, out):
     nc = tc.nc
     with ExitStack() as ctx:
         sb = ctx.enter_context(tc.tile_pool(name="sb", bufs=1))
+        laid = ctx.enter_context(tc.tile_pool(name="laid", bufs=1))
         ps = ctx.enter_context(tc.psum_pool(name="ps", bufs=1))
 
         offsets = sb.tile([P, SLOTS // 16], U16, name="offsets")
         scale_pool = sb.tile([P, POOL], U8, name="scale_pool", align_bytes=64)
         word_pool = sb.tile([P, POOL], I32, name="word_pool", align_bytes=64)
-        q_raw = [sb.tile([P, PACK, QUERIES], F32, name="q_raw%d" % g, tag="raw%d" % g, align_bytes=64) for g in range(PASSES)]
+        q_raw = [laid.tile([P, PACK, QUERIES], F32, name="q_raw%d" % g, offset=(1024, 5120)[g], align_bytes=64) for g in range(PASSES)]
 
         nc.vector.memset(scale_pool[:].bitcast(I32), 0)
         words = k_words[0].rearrange("p t b -> p (t b)").bitcast(I32)
-        nc.sync.dma_start(offsets[:], offs)
         nc.sync.dma_start(out=word_pool[:, 0:LEAD], in_=words[:, 0:LEAD])
+        nc.sync.dma_start(offsets[:], offs)
         nc.sync.dma_start(
             out=scale_pool[QUAD : 3 * QUAD : 2, :].bitcast(I32),
             in_=k_scales.rearrange("o f t -> f o t").bitcast(I32),
@@ -57,17 +58,17 @@ def tile_attend_softmaxsim_kernel(tc, qT, k_words, k_scales, iw, offs, out):
         for h in range(2):
             nc.vector.memset(k_plane[h][:].bitcast(I32), 0)
 
+        scale_listed = [sb.tile([P, HALF], U8, name="scale_listed%d" % h, tag="listed%d" % h, align_bytes=64) for h in range(2)]
         for h in range(2):
-            scale_listed = sb.tile([P, HALF], U8, name="scale_listed%d" % h, align_bytes=64)
             nc.vector.tensor_copy(
-                out=scale_listed[:],
+                out=scale_listed[h][:],
                 in_=scale_pool[:].indirect(offsets[:, h * HALF // 16 : (h + 1) * HALF // 16]),
             )
             for quad in (0, 2, 1, 3):
                 row = QUAD + 16 * quad
                 nc.sync.dma_start(
                     out=k_plane[h][QUAD * quad : QUAD * quad + 4, :].bitcast(I32),
-                    in_=scale_listed[row : row + 16 : 2, :].bitcast(I32),
+                    in_=scale_listed[h][row : row + 16 : 2, :].bitcast(I32),
                 )
 
         q_grouped = [sb.tile([P, QUERIES, PACK], BF16, name="q_grouped%d" % g, tag="grouped%d" % g, align_bytes=64) for g in range(PASSES)]
@@ -86,8 +87,7 @@ def tile_attend_softmaxsim_kernel(tc, qT, k_words, k_scales, iw, offs, out):
                 in_=q_grouped[g][:].rearrange("p w j -> p (w j)"),
             )
 
-        def gather(h, tag):
-            listed = sb.tile([P, HALF], U32, name="pairs%d" % h, tag=tag, align_bytes=64)
+        def gather(h, listed):
             nc.vector.tensor_copy(
                 out=listed[:],
                 in_=word_pool[:].bitcast(U32).indirect(offsets[:, h * HALF // 16 : (h + 1) * HALF // 16]),
@@ -116,8 +116,8 @@ def tile_attend_softmaxsim_kernel(tc, qT, k_words, k_scales, iw, offs, out):
                 op=mybir.AluOpType.max,
             )
 
-        front_bank = ps.tile([P, 512], F32, name="front_bank")
-        pairs = gather(0, "pairs0")
+        front_banks = [ps.tile([P, 128], F32, name="front_bank%d" % i) for i in range(4)]
+        pairs = gather(0, sb.tile([P, HALF], U32, name="pairs0", align_bytes=64))
         quantise(0)
         warm_bank = ps.tile([P, 512], F32, name="warm_bank")
         nc.tensor.matmul_mx(
@@ -125,25 +125,28 @@ def tile_attend_softmaxsim_kernel(tc, qT, k_words, k_scales, iw, offs, out):
             lhsT=q_codes[0][:].bitcast(FP8X4),
             lhsT_scale=q_plane[0][:],
             rhs=pairs[:, 0:256].bitcast(FP4X4),
-            rhs_scale=k_plane[0][:, 0:512],
+            rhs_scale=scale_listed[0][:],
             start=True,
             stop=True,
         )
-        front = sb.tile([P, PASSES, 2 * HALF], U8, name="front", tag="raw0", align_bytes=64)
         halves = pairs[:].bitcast(U16).rearrange("p (n g) -> p g n", g=PASSES)
-        for g in range(PASSES):
-            nc.vector.tensor_copy(out=front[:, g, :].bitcast(U16), in_=halves[:, g, :])
+        front = [laid.tile([P, 2 * HALF], U8, name="front%d" % g, offset=(512, 4608)[g], align_bytes=64) for g in range(PASSES)]
+        nc.vector.tensor_copy(out=front[0][:].bitcast(U16), in_=halves[:, 0, :])
+        for i in range(4):
+            product(front_banks[i][:], 0, front[0][:, 256 * i : 256 * i + 256], 128 * i, 128, True)
+        pairs = gather(1, laid.tile([P, HALF], U32, name="pairs1", offset=2560, align_bytes=64))
         quantise(1)
-        weight = sb.tile([P, 1], F32, name="weight", tag="grouped0", align_bytes=64)
+        for c in range(2):
+            nc.vector.tensor_copy(out=front[1][:, 512 * c : 512 * c + 512].bitcast(U16), in_=halves[:, 1, 256 * c : 256 * c + 256])
+        for i in range(4):
+            product(front_banks[i][:], 1, front[1][:, 256 * i : 256 * i + 256], 128 * i, 128, False)
+        weight = sb.tile([P, 1], F32, name="weight", tag="listed1", align_bytes=64)
         nc.sync.dma_start(out=weight[:], in_=iw[0])
-        for g in range(PASSES):
-            product(front_bank[:], g, front[:, g, :], 0, HALF, g == 0)
 
-        pairs = gather(1, "raw1")
         banks = [ps.tile([P, 512], F32, name="back_bank%d" % i) for i in range(3)]
         place = {0: (0, 0), 128: (0, 128), 256: (1, 0), 384: (2, 0)}
-        for first, n in ((0, 128), (128, 128), (256, 256)):
-            back = sb.tile([P, PASSES, 2 * n], U8, name="back%d" % first, align_bytes=64)
+        for first, n in ((0, 256), (256, 256)):
+            back = laid.tile([P, PASSES, 2 * n], U8, name="back%d" % first, offset=5632 + 4 * first, align_bytes=64)
             nc.vector.tensor_copy(
                 out=back[:].bitcast(U16),
                 in_=pairs[:, first : first + n].bitcast(U16).rearrange("p (n g) -> p g n", g=PASSES),
@@ -153,7 +156,8 @@ def tile_attend_softmaxsim_kernel(tc, qT, k_words, k_scales, iw, offs, out):
                 for g in (1, 0):
                     product(banks[bank][:, at : at + 128], g, back[:, g, 2 * c : 2 * c + 256], HALF + first + c, 128, g == 1)
 
-        largest(front_bank, 0, HALF)
+        for i in range(4):
+            largest(front_banks[i], 128 * i, 128)
         largest(banks[0], HALF, 256)
         largest(banks[1], HALF + 256, 128)
         largest(banks[2], HALF + 384, 128)

@@ -117,30 +117,23 @@ def tile_attend_softmaxsim_kernel(tc, qT, k_words, k_scales, iw, offs, out):
             )
 
         front_banks = [ps.tile([P, 128], F32, name="front_bank%d" % i) for i in range(4)]
-        pairs = gather(0, sb.tile([P, HALF], U32, name="pairs0", align_bytes=64))
+        front_pairs = gather(0, sb.tile([P, HALF], U32, name="pairs0", align_bytes=64))
+        pairs = gather(1, sb.tile([P, HALF], U32, name="pairs1", align_bytes=64))
+        halves = front_pairs[:].bitcast(U16).rearrange("p (n g) -> p g n", g=PASSES)
+        lead = sb.tile([P, 256], U8, name="lead", align_bytes=64)
+        rest = laid.tile([P, 768], U8, name="rest", offset=512, align_bytes=64)
+        second = laid.tile([P, 2 * HALF], U8, name="second", offset=2048, align_bytes=64)
+        nc.vector.tensor_copy(out=lead[:].bitcast(U16), in_=halves[:, 0, 0:128])
         quantise(0)
-        warm_bank = ps.tile([P, 512], F32, name="warm_bank")
-        nc.tensor.matmul_mx(
-            out=warm_bank[:],
-            lhsT=q_codes[0][:].bitcast(FP8X4),
-            lhsT_scale=q_plane[0][:],
-            rhs=pairs[:, 0:256].bitcast(FP4X4),
-            rhs_scale=scale_listed[0][:],
-            start=True,
-            stop=True,
-        )
-        halves = pairs[:].bitcast(U16).rearrange("p (n g) -> p g n", g=PASSES)
-        front = [laid.tile([P, 2 * HALF], U8, name="front%d" % g, offset=(512, 4608)[g], align_bytes=64) for g in range(PASSES)]
-        nc.vector.tensor_copy(out=front[0][:].bitcast(U16), in_=halves[:, 0, :])
-        for i in range(4):
-            product(front_banks[i][:], 0, front[0][:, 256 * i : 256 * i + 256], 128 * i, 128, True)
-        pairs = gather(1, laid.tile([P, HALF], U32, name="pairs1", offset=2560, align_bytes=64))
+        nc.vector.tensor_copy(out=rest[:].bitcast(U16), in_=halves[:, 0, 128:HALF])
+        product(front_banks[0][:], 0, lead[:], 0, 128, True)
+        for i in range(1, 4):
+            product(front_banks[i][:], 0, rest[:, 256 * i - 256 : 256 * i], 128 * i, 128, True)
+        nc.vector.tensor_copy(out=second[:].bitcast(U16), in_=halves[:, 1, :])
         quantise(1)
-        for c in range(2):
-            nc.vector.tensor_copy(out=front[1][:, 512 * c : 512 * c + 512].bitcast(U16), in_=halves[:, 1, 256 * c : 256 * c + 256])
         for i in range(4):
-            product(front_banks[i][:], 1, front[1][:, 256 * i : 256 * i + 256], 128 * i, 128, False)
-        weight = sb.tile([P, 1], F32, name="weight", tag="listed1", align_bytes=64)
+            product(front_banks[i][:], 1, second[:, 256 * i : 256 * i + 256], 128 * i, 128, False)
+        weight = laid.tile([P, 1], F32, name="weight", offset=1536, align_bytes=64)
         nc.sync.dma_start(out=weight[:], in_=iw[0])
 
         banks = [ps.tile([P, 512], F32, name="back_bank%d" % i) for i in range(3)]
@@ -148,8 +141,8 @@ def tile_attend_softmaxsim_kernel(tc, qT, k_words, k_scales, iw, offs, out):
         for first, n in ((0, 256), (256, 256)):
             back = laid.tile([P, PASSES, 2 * n], U8, name="back%d" % first, offset=5632 + 4 * first, align_bytes=64)
             nc.vector.tensor_copy(
-                out=back[:].bitcast(U16),
-                in_=pairs[:, first : first + n].bitcast(U16).rearrange("p (n g) -> p g n", g=PASSES),
+                out=back[:].bitcast(U16).rearrange("p g (c n) -> p c g n", c=2),
+                in_=pairs[:, first : first + n].bitcast(U16).rearrange("p (c n g) -> p c g n", c=2, g=PASSES),
             )
             for c in range(0, n, 128):
                 bank, at = place[first + c]

@@ -116,23 +116,18 @@ def tile_attend_softmaxsim_kernel(tc, qT, k_words, k_scales, iw, offs, out):
                 op=mybir.AluOpType.max,
             )
 
-        front_banks = [ps.tile([P, 128], F32, name="front_bank%d" % i) for i in range(4)]
+        front_bank = ps.tile([P, 512], F32, name="front_bank")
         front_pairs = gather(0, sb.tile([P, HALF], U32, name="pairs0", align_bytes=64))
         pairs = gather(1, sb.tile([P, HALF], U32, name="pairs1", align_bytes=64))
         halves = front_pairs[:].bitcast(U16).rearrange("p (n g) -> p g n", g=PASSES)
-        lead = sb.tile([P, 256], U8, name="lead", align_bytes=64)
-        rest = laid.tile([P, 768], U8, name="rest", offset=512, align_bytes=64)
-        second = laid.tile([P, 2 * HALF], U8, name="second", offset=2048, align_bytes=64)
-        nc.vector.tensor_copy(out=lead[:].bitcast(U16), in_=halves[:, 0, 0:128])
-        quantise(0)
-        nc.vector.tensor_copy(out=rest[:].bitcast(U16), in_=halves[:, 0, 128:HALF])
-        product(front_banks[0][:], 0, lead[:], 0, 128, True)
-        for i in range(1, 4):
-            product(front_banks[i][:], 0, rest[:, 256 * i - 256 : 256 * i], 128 * i, 128, True)
-        nc.vector.tensor_copy(out=second[:].bitcast(U16), in_=halves[:, 1, :])
-        quantise(1)
-        for i in range(4):
-            product(front_banks[i][:], 1, second[:, 256 * i : 256 * i + 256], 128 * i, 128, False)
+        front = [
+            sb.tile([P, 2 * HALF], U8, name="front0", align_bytes=64),
+            laid.tile([P, 2 * HALF], U8, name="front1", offset=2048, align_bytes=64),
+        ]
+        for g in range(PASSES):
+            nc.vector.tensor_copy(out=front[g][:].bitcast(U16), in_=halves[:, g, :])
+            quantise(g)
+            product(front_bank[:], g, front[g][:], 0, HALF, g == 0)
         weight = laid.tile([P, 1], F32, name="weight", offset=1536, align_bytes=64)
         nc.sync.dma_start(out=weight[:], in_=iw[0])
 
@@ -149,8 +144,7 @@ def tile_attend_softmaxsim_kernel(tc, qT, k_words, k_scales, iw, offs, out):
                 for g in (1, 0):
                     product(banks[bank][:, at : at + 128], g, back[:, g, 2 * c : 2 * c + 256], HALF + first + c, 128, g == 1)
 
-        for i in range(4):
-            largest(front_banks[i], 128 * i, 128)
+        largest(front_bank, 0, HALF)
         largest(banks[0], HALF, 256)
         largest(banks[1], HALF + 256, 128)
         largest(banks[2], HALF + 384, 128)

@@ -87,10 +87,10 @@ def tile_attend_softmaxsim_kernel(tc, qT, k_words, k_scales, iw, offs, out):
                 in_=q_grouped[g][:].rearrange("p w j -> p (w j)"),
             )
 
-        def gather(h, listed):
+        def gather(first, n, listed):
             nc.vector.tensor_copy(
                 out=listed[:],
-                in_=word_pool[:].bitcast(U32).indirect(offsets[:, h * HALF // 16 : (h + 1) * HALF // 16]),
+                in_=word_pool[:].bitcast(U32).indirect(offsets[:, first // 16 : (first + n) // 16]),
             )
             return listed
 
@@ -117,8 +117,8 @@ def tile_attend_softmaxsim_kernel(tc, qT, k_words, k_scales, iw, offs, out):
             )
 
         front_bank = ps.tile([P, 512], F32, name="front_bank")
-        front_pairs = gather(0, sb.tile([P, HALF], U32, name="pairs0", align_bytes=64))
-        pairs = gather(1, sb.tile([P, HALF], U32, name="pairs1", align_bytes=64))
+        front_pairs = gather(0, HALF, sb.tile([P, HALF], U32, name="pairs0", align_bytes=64))
+        third_pairs = gather(HALF, 256, sb.tile([P, 256], U32, name="pairs1", align_bytes=64))
         halves = front_pairs[:].bitcast(U16).rearrange("p (n g) -> p g n", g=PASSES)
         front = [
             sb.tile([P, 2 * HALF], U8, name="front0", align_bytes=64),
@@ -131,18 +131,18 @@ def tile_attend_softmaxsim_kernel(tc, qT, k_words, k_scales, iw, offs, out):
         weight = laid.tile([P, 1], F32, name="weight", offset=1536, align_bytes=64)
         nc.sync.dma_start(out=weight[:], in_=iw[0])
 
+        last_pairs = gather(HALF + 256, 256, laid.tile([P, 256], U32, name="pairs2", offset=5120, align_bytes=64))
         banks = [ps.tile([P, 512], F32, name="back_bank%d" % i) for i in range(3)]
-        place = {0: (0, 0), 128: (0, 128), 256: (1, 0), 384: (2, 0)}
-        for first, n in ((0, 256), (256, 256)):
-            back = laid.tile([P, PASSES, 2 * n], U8, name="back%d" % first, offset=5632 + 4 * first, align_bytes=64)
+        for first, pairs, width in ((0, third_pairs, 256), (256, last_pairs, 128)):
+            back = laid.tile([P, PASSES, 512], U8, name="back%d" % first, offset=6144 + 4 * first, align_bytes=64)
             nc.vector.tensor_copy(
                 out=back[:].bitcast(U16).rearrange("p g (c n) -> p c g n", c=2),
-                in_=pairs[:, first : first + n].bitcast(U16).rearrange("p (c n g) -> p c g n", c=2, g=PASSES),
+                in_=pairs[:].bitcast(U16).rearrange("p (c n g) -> p c g n", c=2, g=PASSES),
             )
-            for c in range(0, n, 128):
-                bank, at = place[first + c]
+            for c in range(0, 256, width):
+                bank = banks[first // 256 + c // 128]
                 for g in (1, 0):
-                    product(banks[bank][:, at : at + 128], g, back[:, g, 2 * c : 2 * c + 256], HALF + first + c, 128, g == 1)
+                    product(bank[:, 0:width], g, back[:, g, 2 * c : 2 * (c + width)], HALF + first + c, width, g == 1)
 
         largest(front_bank, 0, HALF)
         largest(banks[0], HALF, 256)

@@ -23,6 +23,7 @@ HALF = SLOTS // 2
 SCALE_ROWS = 16
 QUAD = 32
 LEAD = 1280
+EARLY = 768
 
 FLOPS = 2 * PASSES * K_PASS * QUERIES * SLOTS
 
@@ -89,10 +90,9 @@ def tile_attend_softmaxsim_kernel(tc, qT, k_words, k_scales, iw, offs, out):
 
         def gather(first, n, listed):
             nc.vector.tensor_copy(
-                out=listed[:],
+                out=listed,
                 in_=word_pool[:].bitcast(U32).indirect(offsets[:, first // 16 : (first + n) // 16]),
             )
-            return listed
 
         best = sb.tile([P, SLOTS // RUN], F32, name="best")
         result = sb.tile([P, SLOTS // RUN], F32, name="result")
@@ -116,33 +116,40 @@ def tile_attend_softmaxsim_kernel(tc, qT, k_words, k_scales, iw, offs, out):
                 op=mybir.AluOpType.max,
             )
 
+        def part(out, pairs, g):
+            nc.vector.tensor_copy(
+                out=out[:].bitcast(U16),
+                in_=pairs.bitcast(U16).rearrange("p (n g) -> p g n", g=PASSES)[:, g, :],
+            )
+            return out
+
         front_bank = ps.tile([P, 512], F32, name="front_bank")
-        front_pairs = gather(0, HALF, sb.tile([P, HALF], U32, name="pairs0", align_bytes=64))
-        third_pairs = gather(HALF, 256, sb.tile([P, 256], U32, name="pairs1", align_bytes=64))
-        halves = front_pairs[:].bitcast(U16).rearrange("p (n g) -> p g n", g=PASSES)
-        front = [
-            sb.tile([P, 2 * HALF], U8, name="front0", align_bytes=64),
-            laid.tile([P, 2 * HALF], U8, name="front1", offset=2048, align_bytes=64),
-        ]
-        for g in range(PASSES):
-            nc.vector.tensor_copy(out=front[g][:].bitcast(U16), in_=halves[:, g, :])
-            quantise(g)
-            product(front_bank[:], g, front[g][:], 0, HALF, g == 0)
-        weight = laid.tile([P, 1], F32, name="weight", offset=1536, align_bytes=64)
+        banks = [ps.tile([P, 512], F32, name="back_bank%d" % i) for i in range(3)]
+        pairs = sb.tile([P, EARLY], U32, name="pairs", align_bytes=64)
+        gather(0, HALF, pairs[:, 0:HALF])
+        gather(HALF, 256, pairs[:, HALF:EARLY])
+        front = part(sb.tile([P, 2 * HALF], U8, name="front", align_bytes=64), pairs[:, 0:HALF], 0)
+        quantise(0)
+        product(front_bank[:], 0, front[:], 0, HALF, True)
+        second = part(laid.tile([P, 2 * EARLY], U8, name="second", offset=1536, align_bytes=64), pairs[:], 1)
+        quantise(1)
+        product(front_bank[:], 1, second[:, 0 : 2 * HALF], 0, HALF, False)
+        product(banks[0][:, 0:256], 1, second[:, 2 * HALF : 2 * EARLY], HALF, 256, True)
+        weight = laid.tile([P, 1], F32, name="weight", offset=1024, align_bytes=64)
         nc.sync.dma_start(out=weight[:], in_=iw[0])
 
-        last_pairs = gather(HALF + 256, 256, laid.tile([P, 256], U32, name="pairs2", offset=5120, align_bytes=64))
-        banks = [ps.tile([P, 512], F32, name="back_bank%d" % i) for i in range(3)]
-        for first, pairs, width in ((0, third_pairs, 256), (256, last_pairs, 128)):
-            back = laid.tile([P, PASSES, 512], U8, name="back%d" % first, offset=6144 + 4 * first, align_bytes=64)
-            nc.vector.tensor_copy(
-                out=back[:].bitcast(U16).rearrange("p g (c n) -> p c g n", c=2),
-                in_=pairs[:].bitcast(U16).rearrange("p (c n g) -> p c g n", c=2, g=PASSES),
-            )
-            for c in range(0, 256, width):
-                bank = banks[first // 256 + c // 128]
-                for g in (1, 0):
-                    product(bank[:, 0:width], g, back[:, g, 2 * c : 2 * (c + width)], HALF + first + c, width, g == 1)
+        last_pairs = laid.tile([P, 256], U32, name="last_pairs", offset=5120, align_bytes=64)
+        gather(EARLY, 256, last_pairs[:])
+        third = part(laid.tile([P, 512], U8, name="third", offset=6144, align_bytes=64), pairs[:, HALF:EARLY], 0)
+        product(banks[0][:, 0:256], 0, third[:], HALF, 256, False)
+        back = sb.tile([P, PASSES, 512], U8, name="back", align_bytes=64)
+        nc.vector.tensor_copy(
+            out=back[:].bitcast(U16).rearrange("p g (c n) -> p c g n", c=2),
+            in_=last_pairs[:].bitcast(U16).rearrange("p (c n g) -> p c g n", c=2, g=PASSES),
+        )
+        for c in range(2):
+            for g in (1, 0):
+                product(banks[1 + c][:, 0:128], g, back[:, g, 256 * c : 256 * (c + 1)], EARLY + 128 * c, 128, g == 1)
 
         largest(front_bank, 0, HALF)
         largest(banks[0], HALF, 256)

@@ -22,7 +22,7 @@ RUN = 16
 HALF = SLOTS // 2
 SCALE_ROWS = 16
 QUAD = 32
-LEAD = 1280
+LEAD = 1024
 EARLY = 768
 
 FLOPS = 2 * PASSES * K_PASS * QUERIES * SLOTS

@@ -22,7 +22,6 @@ RUN = 16
 HALF = SLOTS // 2
 SCALE_ROWS = 16
 QUAD = 32
-LEAD = 1024
 EARLY = 768
 
 FLOPS = 2 * PASSES * K_PASS * QUERIES * SLOTS
@@ -42,13 +41,13 @@ def tile_attend_softmaxsim_kernel(tc, qT, k_words, k_scales, iw, offs, out):
 
         nc.vector.memset(scale_pool[:].bitcast(I32), 0)
         words = k_words[0].rearrange("p t b -> p (t b)").bitcast(I32)
-        nc.sync.dma_start(out=word_pool[:, 0:LEAD], in_=words[:, 0:LEAD])
+        nc.sync.dma_start(out=word_pool[0:P:2, :], in_=words[0:P:2, :])
         nc.sync.dma_start(offsets[:], offs)
         nc.sync.dma_start(
             out=scale_pool[QUAD : 3 * QUAD : 2, :].bitcast(I32),
             in_=k_scales.rearrange("o f t -> f o t").bitcast(I32),
         )
-        nc.sync.dma_start(out=word_pool[:, LEAD:POOL], in_=words[:, LEAD:POOL])
+        nc.sync.dma_start(out=word_pool[1:P:2, :], in_=words[1:P:2, :])
         for g in range(PASSES):
             nc.sync.dma_start(
                 out=q_raw[g][:],

@@ -22,7 +22,8 @@ RUN = 16
 HALF = SLOTS // 2
 SCALE_ROWS = 16
 QUAD = 32
-EARLY = 768
+QUARTER = SLOTS // 4
+EARLY = 3 * QUARTER
 
 FLOPS = 2 * PASSES * K_PASS * QUERIES * SLOTS
 
@@ -122,37 +123,39 @@ def tile_attend_softmaxsim_kernel(tc, qT, k_words, k_scales, iw, offs, out):
             )
             return out
 
-        front_bank = ps.tile([P, 512], F32, name="front_bank")
-        banks = [ps.tile([P, 512], F32, name="back_bank%d" % i) for i in range(3)]
+        banks = [ps.tile([P, 512], F32, name="bank%d" % i) for i in range(5)]
         pairs = sb.tile([P, EARLY], U32, name="pairs", align_bytes=64)
         gather(0, HALF, pairs[:, 0:HALF])
-        gather(HALF, 256, pairs[:, HALF:EARLY])
-        front = part(sb.tile([P, 2 * HALF], U8, name="front", align_bytes=64), pairs[:, 0:HALF], 0)
+        gather(HALF, QUARTER, pairs[:, HALF:EARLY])
+        front0 = part(sb.tile([P, 2 * HALF], U8, name="front0", align_bytes=64), pairs[:, 0:HALF], 0)
         quantise(0)
-        product(front_bank[:], 0, front[:], 0, HALF, True)
-        second = part(laid.tile([P, 2 * EARLY], U8, name="second", offset=1536, align_bytes=64), pairs[:], 1)
+        for c in range(2):
+            product(banks[c][:, 0:QUARTER], 0, front0[:, 2 * QUARTER * c : 2 * QUARTER * (c + 1)], QUARTER * c, QUARTER, True)
+        third0 = part(laid.tile([P, 2 * QUARTER], U8, name="third0", offset=1536, align_bytes=64), pairs[:, HALF:EARLY], 0)
+        product(banks[2][:, 0:QUARTER], 0, third0[:], HALF, QUARTER, True)
+        front1 = part(laid.tile([P, 2 * HALF], U8, name="front1", offset=2048, align_bytes=64), pairs[:, 0:HALF], 1)
         quantise(1)
-        product(front_bank[:], 1, second[:, 0 : 2 * HALF], 0, HALF, False)
-        product(banks[0][:, 0:256], 1, second[:, 2 * HALF : 2 * EARLY], HALF, 256, True)
+        for c in range(2):
+            product(banks[c][:, 0:QUARTER], 1, front1[:, 2 * QUARTER * c : 2 * QUARTER * (c + 1)], QUARTER * c, QUARTER, False)
         weight = laid.tile([P, 1], F32, name="weight", offset=1024, align_bytes=64)
         nc.sync.dma_start(out=weight[:], in_=iw[0])
 
-        last_pairs = laid.tile([P, 256], U32, name="last_pairs", offset=5120, align_bytes=64)
-        gather(EARLY, 256, last_pairs[:])
-        third = part(laid.tile([P, 512], U8, name="third", offset=6144, align_bytes=64), pairs[:, HALF:EARLY], 0)
-        product(banks[0][:, 0:256], 0, third[:], HALF, 256, False)
-        back = sb.tile([P, PASSES, 512], U8, name="back", align_bytes=64)
+        last_pairs = laid.tile([P, QUARTER], U32, name="last_pairs", offset=5120, align_bytes=64)
+        gather(EARLY, QUARTER, last_pairs[:])
+        third1 = part(laid.tile([P, 2 * QUARTER], U8, name="third1", offset=6144, align_bytes=64), pairs[:, HALF:EARLY], 1)
+        product(banks[2][:, 0:QUARTER], 1, third1[:], HALF, QUARTER, False)
+        back = sb.tile([P, PASSES, 2 * QUARTER], U8, name="back", align_bytes=64)
         nc.vector.tensor_copy(
             out=back[:].bitcast(U16).rearrange("p g (c n) -> p c g n", c=2),
             in_=last_pairs[:].bitcast(U16).rearrange("p (c n g) -> p c g n", c=2, g=PASSES),
         )
         for c in range(2):
             for g in (1, 0):
-                product(banks[1 + c][:, 0:128], g, back[:, g, 256 * c : 256 * (c + 1)], EARLY + 128 * c, 128, g == 1)
+                product(banks[3 + c][:, 0:128], g, back[:, g, 256 * c : 256 * (c + 1)], EARLY + 128 * c, 128, g == 1)
 
-        largest(front_bank, 0, HALF)
-        largest(banks[0], HALF, 256)
-        largest(banks[1], HALF + 256, 128)
-        largest(banks[2], HALF + 384, 128)
+        for c in range(3):
+            largest(banks[c], QUARTER * c, QUARTER)
+        for c in range(2):
+            largest(banks[3 + c], EARLY + 128 * c, 128)
         nc.vector.tensor_scalar_mul(result[:], best[:], weight[:, 0:1])
         nc.sync.dma_start(out=out[0], in_=result[:])

@@ -24,6 +24,7 @@ SCALE_ROWS = 16
 QUAD = 32
 QUARTER = SLOTS // 4
 EARLY = 3 * QUARTER
+SCALAR_SHARE = 80
 
 FLOPS = 2 * PASSES * K_PASS * QUERIES * SLOTS
 
@@ -75,10 +76,21 @@ def tile_attend_softmaxsim_kernel(tc, qT, k_words, k_scales, iw, offs, out):
         q_grouped = [sb.tile([P, QUERIES, PACK], BF16, name="q_grouped%d" % g, tag="grouped%d" % g, align_bytes=64) for g in range(PASSES)]
         q_codes = [sb.tile([P, QUERIES], U32, name="q_codes%d" % g, align_bytes=64) for g in range(PASSES)]
         q_plane = [sb.tile([P, QUERIES], U8, name="q_plane%d" % g, align_bytes=64) for g in range(PASSES)]
-        for g in range(PASSES):
+        def walk(tile, pattern, first, last):
+            return tile[:].rearrange(pattern, i=4)[:, first // 4 : last // 4]
+
+        nc.gpsimd.tensor_scalar(
+            out=walk(q_grouped[0], "p (c i) t -> p c t i", SCALAR_SHARE, QUERIES),
+            in0=walk(q_raw[0], "p t (c i) -> p c t i", SCALAR_SHARE, QUERIES),
+            scalar1=1.0,
+            scalar2=0.0,
+            op0=mybir.AluOpType.mult,
+            op1=mybir.AluOpType.add,
+        )
+        for g, last in enumerate((SCALAR_SHARE, QUERIES)):
             nc.scalar.copy(
-                out=q_grouped[g][:].rearrange("p (c i) t -> p c t i", i=4),
-                in_=q_raw[g][:].rearrange("p t (c i) -> p c t i", i=4),
+                out=walk(q_grouped[g], "p (c i) t -> p c t i", 0, last),
+                in_=walk(q_raw[g], "p t (c i) -> p c t i", 0, last),
             )
 
         def quantise(g):
@@ -127,13 +139,13 @@ def tile_attend_softmaxsim_kernel(tc, qT, k_words, k_scales, iw, offs, out):
         pairs = sb.tile([P, EARLY], U32, name="pairs", align_bytes=64)
         gather(0, HALF, pairs[:, 0:HALF])
         gather(HALF, QUARTER, pairs[:, HALF:EARLY])
-        front0 = part(sb.tile([P, 2 * HALF], U8, name="front0", align_bytes=64), pairs[:, 0:HALF], 0)
+        first0 = part(sb.tile([P, 2 * QUARTER], U8, name="first0", align_bytes=64), pairs[:, 0:QUARTER], 0)
         quantise(0)
+        product(banks[0][:, 0:QUARTER], 0, first0[:], 0, QUARTER, True)
+        middle0 = part(laid.tile([P, 2 * HALF], U8, name="middle0", offset=1088, align_bytes=64), pairs[:, QUARTER:EARLY], 0)
         for c in range(2):
-            product(banks[c][:, 0:QUARTER], 0, front0[:, 2 * QUARTER * c : 2 * QUARTER * (c + 1)], QUARTER * c, QUARTER, True)
-        third0 = part(laid.tile([P, 2 * QUARTER], U8, name="third0", offset=1536, align_bytes=64), pairs[:, HALF:EARLY], 0)
-        product(banks[2][:, 0:QUARTER], 0, third0[:], HALF, QUARTER, True)
-        front1 = part(laid.tile([P, 2 * HALF], U8, name="front1", offset=2048, align_bytes=64), pairs[:, 0:HALF], 1)
+            product(banks[1 + c][:, 0:QUARTER], 0, middle0[:, 2 * QUARTER * c : 2 * QUARTER * (c + 1)], QUARTER * (c + 1), QUARTER, True)
+        front1 = part(laid.tile([P, 2 * HALF], U8, name="front1", offset=2112, align_bytes=64), pairs[:, 0:HALF], 1)
         quantise(1)
         for c in range(2):
             product(banks[c][:, 0:QUARTER], 1, front1[:, 2 * QUARTER * c : 2 * QUARTER * (c + 1)], QUARTER * c, QUARTER, False)

@@ -56,21 +56,18 @@ def tile_attend_softmaxsim_kernel(tc, qT, k_words, k_scales, iw, offs, out):
                 in_=qT[0, g * K_PASS : (g + 1) * K_PASS, :].rearrange("(p j) w -> p j w", j=PACK),
             )
 
-        k_plane = [sb.tile([P, PASSES * HALF], U8, name="k_plane%d" % h, align_bytes=64) for h in range(2)]
-        for h in range(2):
-            nc.vector.memset(k_plane[h][:].bitcast(I32), 0)
+        k_plane = [sb.tile([P, SLOTS], U8, name="k_plane%d" % g, align_bytes=64) for g in range(PASSES)]
+        for g in range(PASSES):
+            nc.vector.memset(k_plane[g][:].bitcast(I32), 0)
 
-        scale_listed = [sb.tile([P, HALF], U8, name="scale_listed%d" % h, tag="listed%d" % h, align_bytes=64) for h in range(2)]
-        for h in range(2):
-            nc.vector.tensor_copy(
-                out=scale_listed[h][:],
-                in_=scale_pool[:].indirect(offsets[:, h * HALF // 16 : (h + 1) * HALF // 16]),
-            )
-            for quad in (0, 2, 1, 3):
-                row = QUAD + 16 * quad
+        scale_listed = sb.tile([P, SLOTS], U8, name="scale_listed", align_bytes=64)
+        nc.vector.tensor_copy(out=scale_listed[:], in_=scale_pool[:].indirect(offsets[:]))
+        for g in range(PASSES):
+            for r in range(4):
+                row = QUAD + 4 * r + 2 * g
                 nc.sync.dma_start(
-                    out=k_plane[h][QUAD * quad : QUAD * quad + 4, :].bitcast(I32),
-                    in_=scale_listed[h][row : row + 16 : 2, :].bitcast(I32),
+                    out=k_plane[g][r:P:QUAD, :].bitcast(I32),
+                    in_=scale_listed[row : row + 49 : 16, :].bitcast(I32),
                 )
 
         q_grouped = [sb.tile([P, QUERIES, PACK], BF16, name="q_grouped%d" % g, tag="grouped%d" % g, align_bytes=64) for g in range(PASSES)]
@@ -115,7 +112,7 @@ def tile_attend_softmaxsim_kernel(tc, qT, k_words, k_scales, iw, offs, out):
                 lhsT=q_codes[g][:].bitcast(FP8X4),
                 lhsT_scale=q_plane[g][:],
                 rhs=codes.bitcast(FP4X4),
-                rhs_scale=k_plane[first // HALF][:, g * HALF + first % HALF : g * HALF + first % HALF + width],
+                rhs_scale=k_plane[g][:, first : first + width],
                 start=start,
                 stop=not start,
             )

@@ -127,33 +127,45 @@ def tile_attend_softmaxsim_kernel(tc, qT, k_words, k_scales, iw, offs, out):
 
         def part(out, pairs, g):
             nc.vector.tensor_copy(
-                out=out[:].bitcast(U16),
+                out=out[:].rearrange("p a b -> p (a b)").bitcast(U16),
                 in_=pairs.bitcast(U16).rearrange("p (n g) -> p g n", g=PASSES)[:, g, :],
             )
             return out
 
         banks = [ps.tile([P, 512], F32, name="bank%d" % i) for i in range(5)]
+
+        def quarter_pass(c, g, codes):
+            product(banks[c][:, 0:QUARTER], g, codes, QUARTER * c, QUARTER, g == 0)
+
         pairs = sb.tile([P, EARLY], U32, name="pairs", align_bytes=64)
-        gather(0, HALF, pairs[:, 0:HALF])
-        gather(HALF, QUARTER, pairs[:, HALF:EARLY])
-        first0 = part(sb.tile([P, 2 * QUARTER], U8, name="first0", align_bytes=64), pairs[:, 0:QUARTER], 0)
+        halves = pairs[:].bitcast(U16)
+        gather(QUARTER, HALF, pairs[:, QUARTER:EARLY])
+        gather(0, QUARTER, pairs[:, 0:QUARTER])
+        lead = part(sb.tile([P, 2, 2 * QUARTER], U8, name="lead", align_bytes=64), pairs[:, QUARTER:EARLY], 0)
         quantise(0)
-        product(banks[0][:, 0:QUARTER], 0, first0[:], 0, QUARTER, True)
-        middle0 = part(laid.tile([P, 2 * HALF], U8, name="middle0", offset=1088, align_bytes=64), pairs[:, QUARTER:EARLY], 0)
         for c in range(2):
-            product(banks[1 + c][:, 0:QUARTER], 0, middle0[:, 2 * QUARTER * c : 2 * QUARTER * (c + 1)], QUARTER * (c + 1), QUARTER, True)
-        front1 = part(laid.tile([P, 2 * HALF], U8, name="front1", offset=2112, align_bytes=64), pairs[:, 0:HALF], 1)
+            quarter_pass(1 + c, 0, lead[:, c, :])
+        mixed = laid.tile([P, 2, 2 * QUARTER], U8, name="mixed", offset=1088, align_bytes=64)
+        nc.vector.tensor_copy(
+            out=mixed[:].bitcast(U16),
+            in_=halves[:, 0 : 2 * (HALF + 1)].rearrange("p (a b) -> p a b", a=2)[:, :, 0:HALF:2],
+        )
+        quarter_pass(0, 0, mixed[:, 0, :])
+        last_pairs = laid.tile([P, QUARTER], U32, name="last_pairs", offset=2112, align_bytes=64)
+        gather(EARLY, QUARTER, last_pairs[:])
         quantise(1)
-        for c in range(2):
-            product(banks[c][:, 0:QUARTER], 1, front1[:, 2 * QUARTER * c : 2 * QUARTER * (c + 1)], QUARTER * c, QUARTER, False)
+        quarter_pass(1, 1, mixed[:, 1, :])
         weight = laid.tile([P, 1], F32, name="weight", offset=1024, align_bytes=64)
         nc.sync.dma_start(out=weight[:], in_=iw[0])
 
-        last_pairs = laid.tile([P, QUARTER], U32, name="last_pairs", offset=5120, align_bytes=64)
-        gather(EARLY, QUARTER, last_pairs[:])
-        third1 = part(laid.tile([P, 2 * QUARTER], U8, name="third1", offset=6144, align_bytes=64), pairs[:, HALF:EARLY], 1)
-        product(banks[2][:, 0:QUARTER], 1, third1[:], HALF, QUARTER, False)
-        back = sb.tile([P, PASSES, 2 * QUARTER], U8, name="back", align_bytes=64)
+        rest = laid.tile([P, 2, 2 * QUARTER], U8, name="rest", offset=5120, align_bytes=64)
+        nc.vector.tensor_copy(
+            out=rest[:].bitcast(U16),
+            in_=halves.rearrange("p (a b) -> p a b", a=3)[:, 0:3:2, 1:HALF:2],
+        )
+        for c in range(2):
+            quarter_pass(2 * c, 1, rest[:, c, :])
+        back = laid.tile([P, PASSES, 2 * QUARTER], U8, name="back", offset=6144, align_bytes=64)
         nc.vector.tensor_copy(
             out=back[:].bitcast(U16).rearrange("p g (c n) -> p c g n", c=2),
             in_=last_pairs[:].bitcast(U16).rearrange("p (c n g) -> p c g n", c=2, g=PASSES),
@@ -162,7 +174,7 @@ def tile_attend_softmaxsim_kernel(tc, qT, k_words, k_scales, iw, offs, out):
             for g in (1, 0):
                 product(banks[3 + c][:, 0:128], g, back[:, g, 256 * c : 256 * (c + 1)], EARLY + 128 * c, 128, g == 1)
 
-        for c in range(3):
+        for c in (1, 0, 2):
             largest(banks[c], QUARTER * c, QUARTER)
         for c in range(2):
             largest(banks[3 + c], EARLY + 128 * c, 128)

@@ -24,7 +24,7 @@ SCALE_ROWS = 16
 QUAD = 32
 QUARTER = SLOTS // 4
 EARLY = 3 * QUARTER
-SCALAR_SHARE = 80
+SCALAR_SHARE = 88
 
 FLOPS = 2 * PASSES * K_PASS * QUERIES * SLOTS
 
@@ -73,12 +73,9 @@ def tile_attend_softmaxsim_kernel(tc, qT, k_words, k_scales, iw, offs, out):
         q_grouped = [sb.tile([P, QUERIES, PACK], BF16, name="q_grouped%d" % g, tag="grouped%d" % g, align_bytes=64) for g in range(PASSES)]
         q_codes = [sb.tile([P, QUERIES], U32, name="q_codes%d" % g, align_bytes=64) for g in range(PASSES)]
         q_plane = [sb.tile([P, QUERIES], U8, name="q_plane%d" % g, align_bytes=64) for g in range(PASSES)]
-        def walk(tile, pattern, first, last):
-            return tile[:].rearrange(pattern, i=4)[:, first // 4 : last // 4]
-
         nc.gpsimd.tensor_scalar(
-            out=walk(q_grouped[0], "p (c i) t -> p c t i", SCALAR_SHARE, QUERIES),
-            in0=walk(q_raw[0], "p t (c i) -> p c t i", SCALAR_SHARE, QUERIES),
+            out=q_grouped[0][:, SCALAR_SHARE:QUERIES, :],
+            in0=q_raw[0][:].rearrange("p t w -> p w t")[:, SCALAR_SHARE:QUERIES, :],
             scalar1=1.0,
             scalar2=0.0,
             op0=mybir.AluOpType.mult,
@@ -86,8 +83,8 @@ def tile_attend_softmaxsim_kernel(tc, qT, k_words, k_scales, iw, offs, out):
         )
         for g, last in enumerate((SCALAR_SHARE, QUERIES)):
             nc.scalar.copy(
-                out=walk(q_grouped[g], "p (c i) t -> p c t i", 0, last),
-                in_=walk(q_raw[g], "p t (c i) -> p c t i", 0, last),
+                out=q_grouped[g][:].rearrange("p (c i) t -> p c t i", i=4)[:, 0 : last // 4],
+                in_=q_raw[g][:].rearrange("p t (c i) -> p c t i", i=4)[:, 0 : last // 4],
             )
 
         def quantise(g):

@@ -56,19 +56,25 @@ def tile_attend_softmaxsim_kernel(tc, qT, k_words, k_scales, iw, offs, out):
                 in_=qT[0, g * K_PASS : (g + 1) * K_PASS, :].rearrange("(p j) w -> p j w", j=PACK),
             )
 
-        k_plane = [sb.tile([P, SLOTS], U8, name="k_plane%d" % g, align_bytes=64) for g in range(PASSES)]
-        for g in range(PASSES):
-            nc.vector.memset(k_plane[g][:].bitcast(I32), 0)
+        front = sb.tile([P, PASSES, EARLY], U8, name="front", align_bytes=64)
+        late = sb.tile([P, PASSES, QUARTER], U8, name="late", align_bytes=64)
+        for planes in (front, late):
+            nc.vector.memset(planes[:].rearrange("p g n -> p (g n)").bitcast(I32), 0)
 
         scale_listed = sb.tile([P, SLOTS], U8, name="scale_listed", align_bytes=64)
         nc.vector.tensor_copy(out=scale_listed[:], in_=scale_pool[:].indirect(offsets[:]))
-        for g in range(PASSES):
-            for r in range(4):
-                row = QUAD + 4 * r + 2 * g
+        for planes, first, last in ((front, 0, EARLY), (late, EARLY, SLOTS)):
+            for quad in (0, 2, 1, 3):
+                row = QUAD + 16 * quad
                 nc.sync.dma_start(
-                    out=k_plane[g][r:P:QUAD, :].bitcast(I32),
-                    in_=scale_listed[row : row + 49 : 16, :].bitcast(I32),
+                    out=planes[QUAD * quad : QUAD * quad + 4].rearrange("p g n -> p (g n)").bitcast(I32),
+                    in_=scale_listed[row : row + 16 : 2, first:last].bitcast(I32),
                 )
+
+        def key_plane(g, first, width):
+            if first < EARLY:
+                return front[:, g, first : first + width]
+            return late[:, g, first - EARLY : first - EARLY + width]
 
         q_grouped = [sb.tile([P, QUERIES, PACK], BF16, name="q_grouped%d" % g, tag="grouped%d" % g, align_bytes=64) for g in range(PASSES)]
         q_codes = [sb.tile([P, QUERIES], U32, name="q_codes%d" % g, align_bytes=64) for g in range(PASSES)]
@@ -109,7 +115,7 @@ def tile_attend_softmaxsim_kernel(tc, qT, k_words, k_scales, iw, offs, out):
                 lhsT=q_codes[g][:].bitcast(FP8X4),
                 lhsT_scale=q_plane[g][:],
                 rhs=codes.bitcast(FP4X4),
-                rhs_scale=k_plane[g][:, first : first + width],
+                rhs_scale=key_plane(g, first, width),
                 start=start,
                 stop=not start,
             )

@@ -61,12 +61,17 @@ def tile_attend_softmaxsim_kernel(tc, qT, k_words, k_scales, iw, offs, out):
         for planes in (front, late):
             nc.vector.memset(planes[:].rearrange("p g n -> p (g n)").bitcast(I32), 0)
 
+        idle = sb.tile([P, 2], F32, name="idle")
+        idle_copy = sb.tile([P, 2], BF16, name="idle_copy")
+        nc.gpsimd.memset(idle[:], 0.0)
+        nc.scalar.copy(out=idle_copy[:], in_=idle[:])
+
         scale_listed = sb.tile([P, SLOTS], U8, name="scale_listed", align_bytes=64)
         nc.vector.tensor_copy(out=scale_listed[:], in_=scale_pool[:].indirect(offsets[:]))
-        for planes, first, last in ((front, 0, EARLY), (late, EARLY, SLOTS)):
+        for queue, planes, first, last in ((nc.scalar, front, 0, EARLY), (nc.sync, late, EARLY, SLOTS)):
             for quad in (0, 2, 1, 3):
                 row = QUAD + 16 * quad
-                nc.sync.dma_start(
+                queue.dma_start(
                     out=planes[QUAD * quad : QUAD * quad + 4].rearrange("p g n -> p (g n)").bitcast(I32),
                     in_=scale_listed[row : row + 16 : 2, first:last].bitcast(I32),
                 )

from contextlib import ExitStack

import concourse.mybir as mybir

F32 = mybir.dt.float32
BF16 = mybir.dt.bfloat16
I32 = mybir.dt.int32
U32 = mybir.dt.uint32
U16 = mybir.dt.uint16
U8 = mybir.dt.uint8
FP8X4 = mybir.dt.float8_e4m3fn_x4
FP4X4 = mybir.dt.float4_e2m1fn_x4

P = 128
PACK = 4
K_PASS = P * PACK
PASSES = 2
POOL = 4096
SLOTS = 1024
QUERIES = 128
RUN = 16
HALF = SLOTS // 2
SCALE_ROWS = 16
QUAD = 32
QUARTER = SLOTS // 4
EARLY = 3 * QUARTER
SCALAR_SHARE = 88

FLOPS = 2 * PASSES * K_PASS * QUERIES * SLOTS


def tile_attend_softmaxsim_kernel(tc, qT, k_words, k_scales, iw, offs, out):
    nc = tc.nc
    with ExitStack() as ctx:
        sb = ctx.enter_context(tc.tile_pool(name="sb", bufs=1))
        laid = ctx.enter_context(tc.tile_pool(name="laid", bufs=1))
        ps = ctx.enter_context(tc.psum_pool(name="ps", bufs=1))

        offsets = sb.tile([P, SLOTS // 16], U16, name="offsets")
        scale_pool = sb.tile([P, POOL], U8, name="scale_pool", align_bytes=64)
        word_pool = sb.tile([P, POOL], I32, name="word_pool", align_bytes=64)
        q_raw = [laid.tile([P, PACK, QUERIES], F32, name="q_raw%d" % g, offset=(1024, 5120)[g], align_bytes=64) for g in range(PASSES)]

        nc.vector.memset(scale_pool[:].bitcast(I32), 0)
        words = k_words[0].rearrange("p t b -> p (t b)").bitcast(I32)
        nc.sync.dma_start(out=word_pool[0:P:2, :], in_=words[0:P:2, :])
        nc.sync.dma_start(offsets[:], offs)
        nc.sync.dma_start(
            out=scale_pool[QUAD : 3 * QUAD : 2, :].bitcast(I32),
            in_=k_scales.rearrange("o f t -> f o t").bitcast(I32),
        )
        nc.sync.dma_start(out=word_pool[1:P:2, :], in_=words[1:P:2, :])
        for g in range(PASSES):
            nc.sync.dma_start(
                out=q_raw[g][:],
                in_=qT[0, g * K_PASS : (g + 1) * K_PASS, :].rearrange("(p j) w -> p j w", j=PACK),
            )

        front = sb.tile([P, PASSES, EARLY], U8, name="front", align_bytes=64)
        late = sb.tile([P, PASSES, QUARTER], U8, name="late", align_bytes=64)
        for planes in (front, late):
            nc.vector.memset(planes[:].rearrange("p g n -> p (g n)").bitcast(I32), 0)

        idle = sb.tile([P, 2], F32, name="idle")
        idle_copy = sb.tile([P, 2], BF16, name="idle_copy")
        nc.gpsimd.memset(idle[:], 0.0)
        nc.scalar.copy(out=idle_copy[:], in_=idle[:])

        scale_listed = sb.tile([P, SLOTS], U8, name="scale_listed", align_bytes=64)
        nc.vector.tensor_copy(out=scale_listed[:], in_=scale_pool[:].indirect(offsets[:]))
        for queue, planes, first, last in ((nc.scalar, front, 0, EARLY), (nc.sync, late, EARLY, SLOTS)):
            for quad in (0, 2, 1, 3):
                row = QUAD + 16 * quad
                queue.dma_start(
                    out=planes[QUAD * quad : QUAD * quad + 4].rearrange("p g n -> p (g n)").bitcast(I32),
                    in_=scale_listed[row : row + 16 : 2, first:last].bitcast(I32),
                )

        def key_plane(g, first, width):
            if first < EARLY:
                return front[:, g, first : first + width]
            return late[:, g, first - EARLY : first - EARLY + width]

        q_grouped = [sb.tile([P, QUERIES, PACK], BF16, name="q_grouped%d" % g, tag="grouped%d" % g, align_bytes=64) for g in range(PASSES)]
        q_codes = [sb.tile([P, QUERIES], U32, name="q_codes%d" % g, align_bytes=64) for g in range(PASSES)]
        q_plane = [sb.tile([P, QUERIES], U8, name="q_plane%d" % g, align_bytes=64) for g in range(PASSES)]
        nc.gpsimd.tensor_scalar(
            out=q_grouped[0][:, SCALAR_SHARE:QUERIES, :],
            in0=q_raw[0][:].rearrange("p t w -> p w t")[:, SCALAR_SHARE:QUERIES, :],
            scalar1=1.0,
            scalar2=0.0,
            op0=mybir.AluOpType.mult,
            op1=mybir.AluOpType.add,
        )
        for g, last in enumerate((SCALAR_SHARE, QUERIES)):
            nc.scalar.copy(
                out=q_grouped[g][:].rearrange("p (c i) t -> p c t i", i=4)[:, 0 : last // 4],
                in_=q_raw[g][:].rearrange("p t (c i) -> p c t i", i=4)[:, 0 : last // 4],
            )

        def quantise(g):
            nc.vector.quantize_mx(
                out=q_codes[g][:].bitcast(FP8X4),
                scales=q_plane[g][:],
                in_=q_grouped[g][:].rearrange("p w j -> p (w j)"),
            )

        def gather(first, n, listed):
            nc.vector.tensor_copy(
                out=listed,
                in_=word_pool[:].bitcast(U32).indirect(offsets[:, first // 16 : (first + n) // 16]),
            )

        best = sb.tile([P, SLOTS // RUN], F32, name="best")
        result = sb.tile([P, SLOTS // RUN], F32, name="result")

        def product(bank, g, codes, first, width, start):
            nc.tensor.matmul_mx(
                out=bank,
                lhsT=q_codes[g][:].bitcast(FP8X4),
                lhsT_scale=q_plane[g][:],
                rhs=codes.bitcast(FP4X4),
                rhs_scale=key_plane(g, first, width),
                start=start,
                stop=not start,
            )

        def largest(bank, first, n):
            nc.vector.tensor_reduce(
                out=best[:, first // RUN : (first + n) // RUN],
                in_=bank[:, 0:n].rearrange("p (j r) -> p j r", r=RUN),
                axis=mybir.AxisListType.X,
                op=mybir.AluOpType.max,
            )

        def part(out, pairs, g):
            nc.vector.tensor_copy(
                out=out[:].rearrange("p a b -> p (a b)").bitcast(U16),
                in_=pairs.bitcast(U16).rearrange("p (n g) -> p g n", g=PASSES)[:, g, :],
            )
            return out

        banks = [ps.tile([P, 512], F32, name="bank%d" % i) for i in range(5)]

        def quarter_pass(c, g, codes):
            product(banks[c][:, 0:QUARTER], g, codes, QUARTER * c, QUARTER, g == 0)

        pairs = sb.tile([P, EARLY], U32, name="pairs", align_bytes=64)
        halves = pairs[:].bitcast(U16)
        gather(QUARTER, HALF, pairs[:, QUARTER:EARLY])
        gather(0, QUARTER, pairs[:, 0:QUARTER])
        lead = part(sb.tile([P, 2, 2 * QUARTER], U8, name="lead", align_bytes=64), pairs[:, QUARTER:EARLY], 0)
        quantise(0)
        for c in range(2):
            quarter_pass(1 + c, 0, lead[:, c, :])
        mixed = laid.tile([P, 2, 2 * QUARTER], U8, name="mixed", offset=1088, align_bytes=64)
        nc.vector.tensor_copy(
            out=mixed[:].bitcast(U16),
            in_=halves[:, 0 : 2 * (HALF + 1)].rearrange("p (a b) -> p a b", a=2)[:, :, 0:HALF:2],
        )
        quarter_pass(0, 0, mixed[:, 0, :])
        last_pairs = laid.tile([P, QUARTER], U32, name="last_pairs", offset=2112, align_bytes=64)
        gather(EARLY, QUARTER, last_pairs[:])
        quantise(1)
        quarter_pass(1, 1, mixed[:, 1, :])
        weight = laid.tile([P, 1], F32, name="weight", offset=1024, align_bytes=64)
        nc.sync.dma_start(out=weight[:], in_=iw[0])

        rest = laid.tile([P, 2, 2 * QUARTER], U8, name="rest", offset=5120, align_bytes=64)
        nc.vector.tensor_copy(
            out=rest[:].bitcast(U16),
            in_=halves.rearrange("p (a b) -> p a b", a=3)[:, 0:3:2, 1:HALF:2],
        )
        for c in range(2):
            quarter_pass(2 * c, 1, rest[:, c, :])
        back = laid.tile([P, PASSES, 2 * QUARTER], U8, name="back", offset=6144, align_bytes=64)
        nc.vector.tensor_copy(
            out=back[:].bitcast(U16).rearrange("p g (c n) -> p c g n", c=2),
            in_=last_pairs[:].bitcast(U16).rearrange("p (c n g) -> p c g n", c=2, g=PASSES),
        )
        for c in range(2):
            for g in (1, 0):
                product(banks[3 + c][:, 0:128], g, back[:, g, 256 * c : 256 * (c + 1)], EARLY + 128 * c, 128, g == 1)

        for c in (1, 0, 2):
            largest(banks[c], QUARTER * c, QUARTER)
        for c in range(2):
            largest(banks[3 + c], EARLY + 128 * c, 128)
        nc.vector.tensor_scalar_mul(result[:], best[:], weight[:, 0:1])
        nc.sync.dma_start(out=out[0], in_=result[:])
